import numpy as np, ml_dtypes
CORES = [16,17,18,19,32,33,34,35]
N = 8
import mx_ref
BF = ml_dtypes.bfloat16
def entries(a):
    return np.ascontiguousarray(a.T).reshape(-1)
def table(e):
    return np.ascontiguousarray(np.reshape(e, (-1, 16)).T).astype(np.int32)
def gentries(a):
    return np.ascontiguousarray(a.reshape(8, 16, -1).transpose(0, 2, 1)).reshape(8, -1)
def gtable(e):
    e = np.asarray(e); return np.ascontiguousarray(e.reshape(8, -1, 16).transpose(0, 2, 1)).reshape(128, -1).astype(np.int32)
def tile(rs):
    return np.stack(rs, axis=2).reshape(128, -1).astype(BF)
def pick(q, e):
    c = np.concatenate([q[0].reshape(128, -1, 4), np.zeros((128, 1, 4), np.uint8)], axis=1); s = np.concatenate([q[1], np.ones((16, 1), np.uint8)], axis=1)
    return (np.ascontiguousarray(c[:, e].reshape(128, -1)), np.ascontiguousarray(s[:, e]))
def join(*qs):
    return (np.concatenate([q[0] for q in qs], axis=1), np.concatenate([q[1] for q in qs], axis=1))
def put(q, e, v):
    c, s = q[0].reshape(128, -1, 4).copy(), q[1].copy(); c[:, e] = v[0].reshape(128, -1, 4); s[:, e] = v[1]
    return (c.reshape(128, -1), s)
def pk(c, s):
    return (np.ascontiguousarray(c), mx_ref.live(s))
def emit(q):
    return q[0], q[1]
def packed(v, rng):
    q = [mx_ref.quantize(np.ascontiguousarray(v[r])) for r in range(N)]
    return np.stack([a for a, b in q]), np.stack([mx_ref.plane(b, rng) for a, b in q])
def values_of_codes():
    e, c = np.zeros((128, 128, 4), np.float32), np.zeros((128, 2, 4), np.uint8)
    e[np.arange(128), np.arange(128), 0] = 1
    c[:127, :, 0] = np.arange(256).reshape(2, 128).T[:127]
    return mx_ref.matmul(mx_ref.quantize(e.reshape(128, 512).astype(BF)), (c.reshape(128, 8), np.full((16, 2), 127, np.uint8))).T.reshape(-1).astype(np.float64)
CODE_VALUE, SCALE_VALUE = values_of_codes(), 2.0 ** (np.arange(256) - 127.0)
def decode(q):
    return (CODE_VALUE[q[0]].reshape(16, 8, -1, 4) * SCALE_VALUE[q[1]][:, None, :, None] + 0.0).reshape(128, -1).astype(np.float32)
def f(rng, *shape):
    return mx_ref.flush((rng.standard_normal(shape, dtype=np.float32) * np.exp2(rng.integers(-2, 3, shape[:-1] + (1,)))).astype(BF))
def wide(rng, *shape, cols=0):
    v = rng.standard_normal(shape, dtype=np.float32) * np.exp2(rng.integers(-12, 13, shape)).astype(np.float32)
    if cols: v *= np.repeat(np.exp2(rng.integers(-cols, cols + 1, shape[:-2] + (1, shape[-1] // 4))) * (rng.random(shape[:-2] + (1, shape[-1] // 4)) > 0.0625), 4, axis=-1).astype(np.float32)
    return mx_ref.flush(v.astype(BF))
C, T, K, STEPS = 320, 256, 128, 3
MATES = [1, 2, 4]
DECIDE = [16 * i + k for i in range(STEPS) for k in range(2)]
def numbers_of(rng):
    return {"x": np.array(f(rng, N, 128, 4 * C)), "u": np.array(f(rng, N, 128, 512)), "v": np.array(f(rng, N, 128, 512))}
def lists(rng):
    return {"p": np.stack([gtable(np.stack([rng.permutation(C) for g in range(8)])) for r in range(N)]),
            "ln": np.stack([table(np.concatenate([rng.permutation(T) for i in range(STEPS)])) for r in range(N)])}
def layers(rng):
    k = np.exp2(rng.permuted(np.tile(np.arange(128) % 5 - 2.0, (N, 1)), axis=1))[:, :, None]
    return np.array(mx_ref.flush((rng.standard_normal((N, 128, 2048)) * k).astype(np.float32).astype(BF))).reshape(N, 8, 16, 4, 8, 16, 4)
def weights(rng, w):
    c, s = packed(np.ascontiguousarray(w).reshape(N, 128, 2048), rng)
    return {"wc": c, "ws": s}
def setup_inputs(rng):
    return {**numbers_of(rng), **lists(rng), **weights(rng, layers(rng))}
def setup_inputs_ties(rng):
    d = numbers_of(rng)
    x = d["x"].reshape(N, 8, 16, C, 4)
    x[:, :, 0] = 0
    x[:, :, 0, :, 0] = rng.integers(-1, 2, (N, 8, C)).astype(np.float32).astype(BF)
    x[:, :, :, ::8] = 0
    u = d["u"].reshape(N, 128, 128, 4)
    u[:, :, DECIDE] = 0
    o = rng.permutation(N)
    for r in range(N):
        g = rng.permutation(8)
        for i, c in enumerate(DECIDE): u[r, 16 * g[i], c, 0] = 0.0 if r == o[0] else -1.0 if r == o[1] else 1.0
    w = layers(rng)
    w[:, :, 0] = 0
    w[:, :, :, :, :, 0] = 0
    return {"x": x.reshape(N, 128, 4 * C), "u": u.reshape(N, 128, 512), "v": d["v"], **lists(rng), **weights(rng, w)}
def setup_inputs_near(rng):
    d = numbers_of(rng)
    x = d["x"].reshape(N, 8, 16, C, 4)
    u = d["u"].reshape(N, 128, 128, 4)
    x[:, :, :8] = 0
    u[:, :, DECIDE] = 0
    o = rng.permutation(N)
    for r in range(N):
        k = 2.0 ** -30 if o[r] % 2 == 0 else 1.0
        s = rng.integers(-1, 2, (8, C)) * k
        x[r, :, 0, :, 0] = (1.125 * s).astype(np.float32).astype(BF)
        x[r, :, 1, :, 0] = (-s).astype(np.float32).astype(BF)
        for g in rng.permutation(8)[:4]:
            c = rng.integers(T)
            x[r, g, 0, c, 0] = 2.0 ** 16 * rng.choice([-1.0, 1.0])
            x[r, g, 1, c, 0] = 0
        g = rng.permutation(8)
        for i, c in enumerate(DECIDE):
            u[r, 16 * g[i], c, 0] = 1.125 * k
            u[r, 16 * g[i] + 1, c, 0] = 1.25 * k
    w = layers(rng)
    w[:, :, :8] = 0
    w[:, :, :, :, :, :8] = 0
    return {"x": x.reshape(N, 128, 4 * C), "u": u.reshape(N, 128, 512), "v": d["v"], **lists(rng), **weights(rng, w)}
def setup_inputs_twice(rng):
    d = numbers_of(rng)
    x = d["x"].reshape(N, 8, 16, C, 4)
    a = (2 * rng.integers(2, 8, (N, 8, 8, C, 4)) + 1) * np.exp2(rng.integers(-5, -3, (N, 8, 8, C, 4)))
    a[:, :, 0, :, 0] = 1.96875 * 2.0 ** 12
    x[:, :, :8] = (a * rng.choice([-1.0, 1.0], a.shape)).astype(np.float32).astype(BF)
    w = layers(rng)
    w[:, :, 0] = 0
    w[:, :, :, :, :, :8] = 0
    return {"x": x.reshape(N, 128, 4 * C), "u": d["u"], "v": d["v"], **lists(rng), **weights(rng, w)}
def setup_inputs_ends(rng):
    d = numbers_of(rng)
    e = rng.permutation(N) % 4
    x, w = np.zeros((N, 8, 16, C, 4)), np.zeros((N, 128, 4, 128, 4), np.float32)
    u = d["u"].reshape(N, 128, 128, 4)
    v, p, n, j, i = [], [], [], np.arange(C), np.arange(128)
    for r in range(N):
        k = e[r]
        s = rng.choice([-1.0, 1.0], (8, 1, C, 1))
        x[r] = 2.0 ** 17 * (1.0, s[:1], 2.0 ** -47, s)[k]
        for c in DECIDE:
            a = (2.0 ** 30, 0.0, 2.0 ** -30 if c % 16 else -2.0 ** -30, 2.0 ** 30 * rng.choice([-1.0, 1.0], (128, 4)))[k]
            u[r, :, c] = np.asarray(a, np.float32).astype(BF)
        v.append((1.0 if k == 0 else rng.choice([-1.0, 1.0], (128, 512))) * np.full((128, 512), 2.0 ** (-30 if k == 2 else 30)))
        if k == 3:
            for b in range(4): w[r, (i + 16) % 128, b, i, b] = -1024
        else: w[r] = (2, 0, -2)[k]
        p.append(gtable((np.tile(j, (8, 1)), np.tile(j[::-1], (8, 1)), (j + 16 * np.arange(8)[:, None] + 1) % C, np.stack([rng.permutation(C) for g in range(8)]))[k]))
        n.append(table((np.tile(np.arange(T), STEPS), np.tile(np.arange(T)[::-1], STEPS), np.tile(rng.permutation(T), STEPS), np.concatenate([rng.permutation(T) for g in range(STEPS)]))[k]))
    return {"x": x.astype(np.float32).reshape(N, 128, 4 * C).astype(BF), "u": u.reshape(N, 128, 512), "v": np.stack(v).astype(np.float32).astype(BF), "p": np.stack(p), "ln": np.stack(n), **weights(rng, w.astype(BF))}
def setup_inputs_spread(rng):
    d = setup_inputs(rng)
    d["x"] = wide(rng, N, 128, 4 * C, cols=2)
    return d
def check_inputs(d):
    b = []
    for k, most in (("x", 2.0 ** 17), ("u", 2.0 ** 30), ("v", 2.0 ** 30)):
        a = np.abs(d[k].astype(np.float32))
        if not (np.isfinite(a).all() and ((a == 0) | (a >= 2.0 ** -30) & (a <= most)).all()): b.append("a value of " + k)
    none, least, most = [emit(mx_ref.quantize(np.full((128, 16), k, np.float32).astype(BF)))[1][0, 0] for k in (0.0, 2.0 ** -30, 2.0 ** 30)]
    for r in range(N):
        if (np.sort(gentries(d["p"][r]), axis=1) != np.arange(C)).any(): b.append("p: a group's entries aren't a permutation")
        if (np.sort(entries(d["ln"][r]).reshape(STEPS, T), axis=1) != np.arange(T)).any(): b.append("ln: a step's entries aren't a permutation")
        if ((d["wc"][r] & 0x7F) == 0x7F).any(): b.append("wc: a code that is no number")
        s = mx_ref.live(d["ws"][r])
        if ((s != none) & ((s < least) | (s > most))).any(): b.append("ws: a scale out of range")
        with np.errstate(all="ignore"):
            w = np.abs(decode(pk(d["wc"][r], d["ws"][r]))).astype(np.float64).reshape(128, 512, 4)
            if not np.max(np.sum(w, axis=(0, 2))) <= 1024: b.append("W: the sizes of a column add up to more than 1024")
    return b
def moves(s, p, ln):
    at = C * np.arange(8)[:, None] + p
    has = at.copy()
    for i in range(STEPS):
        link = 2 * ln[T * i:T * i + T] + (s[16 * i + 1] > 0)
        push, stack, own = s[16 * i] > 0, has[:, :T].copy(), has[link % 8, T + link // 8]
        has[:, :T] = np.where(push, np.concatenate([own[None], stack[:7]]), np.concatenate([stack[1:], own[None]]))
        has[link % 8, T + link // 8] = np.where(push, stack[7], stack[0])
    m = np.zeros(8 * C, np.int64)
    m[at] = has
    return m
def moved(t, m):
    z = t.reshape(8, 16, C, 4).transpose(0, 2, 1, 3).reshape(8 * C, 16, 4)[m]
    return np.ascontiguousarray(z.reshape(8, C, 16, 4).transpose(0, 2, 1, 3)).reshape(128, 4 * C)
def reference(x, u, v, p, ln, wc, ws):
    qu = [mx_ref.quantize(u[r]) for r in range(N)]
    lay = [pk(wc[r], ws[r]) for r in range(N)]
    now = [x[r] for r in range(N)]
    for a in MATES:
        m, qz = [], []
        for r in range(N):
            s = mx_ref.matmul(qu[r], mx_ref.quantize(np.ascontiguousarray(now[r][:, :4 * T])))
            m.append(moves(s, gentries(p[r]), entries(ln[r])))
            qz.append(mx_ref.quantize(moved(now[r], m[r])))
        for r in range(N):
            h = join(pick(qz[r ^ a], np.arange(K)), pick(qz[r], np.arange(K, C)))
            has = decode(h)
            made = tile([np.maximum(mx_ref.matmul(pick(lay[r], np.arange(128 * b, 128 * b + 128)), h), np.float32(0.0)) * np.float32(0.015625) + has[:, b::4] for b in range(4)])
            now[r] = moved(made, np.argsort(m[r]))
    y, op = np.zeros((N, 128, C), np.float32), np.zeros((N, 8, C), np.float32)
    oc, osc = np.zeros((N, 128, 4 * C), np.uint8), np.zeros((N, 16, C), np.uint8)
    for r in range(N):
        q = mx_ref.quantize(now[r])
        y[r] = mx_ref.matmul(mx_ref.quantize(v[r]), q)
        op[r] = m[r].reshape(8, C)
        oc[r], osc[r] = emit(q)
    return {"y": y, "op": op, "oc": oc, "osc": osc}

@@ -1,0 +1,452 @@
+from concourse.mybir import dt, AluOpType as A, AxisListType, ActivationFunctionType as F
+
+f4, bf, u2, i4, X4, u1 = "float32", "bfloat16", "uint16", "int32", "float8_e4m3fn_x4", "uint8"
+SCRATCH = {}
+
+
+def _add(where, dtype, **kw):
+    for k, n in kw.items():
+        SCRATCH[k] = (where, n if isinstance(n, list) else [128, n], dtype)
+
+
+_add("sbuf", bf, ut=512, vt=512, xn=1280, xt=1280, eb=2048, abF=1024, abI=1024, xg=1280, zg=1280, nt=1024, ya=768, yb=512,
+     win=10240, sg=256, tlF=1024, tlI=1024, tr=1024)
+_add("sbuf", X4, wq=512, wp=512, uq=128, vq=128, eq=512, aqF=256, aqI=256, xq=320, zq=320, nq=256, lc0=128, lc1=128, lc2=128)
+_add("sbuf", u1, wz=512, wpz=512, uz=128, vz=128, ez=512, azF=256, azI=256, xz=320, zz=320, nz=256, lz0=128, lz1=128, lz2=128)
+_add("sbuf", f4, iot=320, lbr=256, m16=320, mask=320, res=320, dg=320, ds=320, cols=64, steps=32, wli=32, k16=4, pv=320, atr=320,
+     apr=320, atf=320, apf=320, tab1=2560, tab2=2560, tabp=2560, af=1280, cc=512, v2=320, lbf=768, lg=768, lgi=768, baseF=8192,
+     baseI=8192, ntb=512, tf=320, rl=1280, yo=320, opb=320, hb=4, w2=20, ty=20, q32F=20, q32I=20, biF=20, biI=20)
+_add("sbuf", i4, lw=48, pw=20, pci=8, ni=20, fb=140, gb=60)
+_add("sbuf", u2, l16=48, p16=20, pi16=20, al16=80, n16F=20, n16I=20, wl16=32, ix=20, pl=20, ofz=80, ofx=80)
+_add("dram", f4, tabd=[16, 2560], tabpd=[16, 2560])
+_add("psum", f4, **{"ps%d" % b: 512 for b in range(8)})
+DSEM = ["dp", "dl", "du", "dv", "dxn", "dxt", "dw", "dbA", "dbB", "dt1", "dt2", "do"]
+SEMAPHORES = ["sv", "ss", "st", "sg", "snt", "ar0", "ar1", "ar2"] + DSEM
+
+
+def _fields(g, link):
+    e, b = {}, [0]
+
+    def add(c, k, i, K, w):
+        e[c, k, i, K] = e.get((c, k, i, K), 0) + w
+
+    add(0, "s", 0, 3, 1); add(0, "b", 0, 3, -2); b[0] += 2
+    add(0, "b", 0, 2, 8); add(0, "s", 0, 2, 16); add(0, "s", 1, 2, 16); b[0] += 64
+    add(1, "b", 1, 2, -128); b[0] += 128
+    beta = g % 2
+    if link: b[0] += 130 * beta
+    else: add(0, "b", 2, 0, 2); add(1, "b", 2, 0, 128)
+    if link or g in (1, 6):
+        add(2, "s", 0, 1, 1 << 14); add(2, "b", 1, 0, 1 << 15); add(2, "b", 0, 1, -(1 << 15)); b[0] += 26 << 14
+    elif g in (0, 2, 5, 7):
+        add(2, "b", 0, 0, 1 << 14); b[0] += 30 << 14
+    else: b[0] += 24 << 14
+    if link:
+        add(1, "s", 1, 0, 2048); add(1, "s", 2, 0, 2048)
+        add(1, "b", 2, 0, -8192 if beta else 8192); b[0] += 8192 * beta
+        add(2, "s", 0, 0, -(1 << 20)); add(2, "s", 2, 0, 5 << 19); b[0] += 18 << 19
+    else:
+        w, c = {0: ((1, 1, -1), 2), 7: ((-1, -1, 1), 3), 1: ((0, 1, 1), 2), 6: ((0, -1, -1), 4),
+                2: ((1, 1, 1), 1), 5: ((-1, -1, -1), 4)}.get(g, ((0, 0, 0), 0))
+        for i in range(3):
+            if w[i]: add(1, "s", i, 0, 512 * w[i])
+            add(2, "s", i, 0, -(1 << 20))
+        b[0] += 512 * c + ((g + 19) << 19)
+        if g == 0: add(1, "s", 2, 0, 8192)
+        if g == 7: add(1, "s", 2, 0, -8192); b[0] += 8192
+    return e, b[0]
+
+
+def _weights(inverse):
+    w, bias = {}, [[0] * 8, [0] * 8]
+    for link in (0, 1):
+        for g in range(8):
+            e, b = _fields(g, link)
+            for (c, k, i, K), x in e.items():
+                slot, j = K, i
+                if inverse:
+                    slot, j = (3, 1, 2, 0)[K], 2 - i
+                    if k == "s": b += x; x = -x
+                w.setdefault((8 * c + 2 * j + (k == "b"), slot, link), [0] * 8)[g] += x
+            bias[link][g] = b
+    return w, bias
+
+
+def rank_program(g, core, T, topo):
+    rank = T.rank_of(core)
+    if rank is None:
+        return
+    eng = {"V": g.vector, "S": g.scalar, "T": g.tensor, "G": g, "Y": g.sync}
+    csem = {"V": "sv", "S": "ss", "T": "st", "G": "sg"}
+    cnt, known, log = {}, {q: {} for q in eng}, {}
+
+    def v(name, c0=0, c1=None, cs=1, p0=0, p1=128, ps=1):
+        if c1 is None: c1 = SCRATCH[name][1][1]
+        return {"a": T[name][p0:p1:ps, c0:c1:cs], "r": [(name, p0, p1, c0, c1, cs)]}
+
+    def ind(w, o):
+        return {"a": w["a"].indirect(o["a"]), "r": w["r"] + o["r"]}
+
+    def cb(w):
+        return {"a": w["a"].bitcast(dt.uint8), "r": w["r"]}
+
+    def cw(w):
+        return {"a": w["a"].bitcast(dt.uint32), "r": w["r"]}
+
+    def ext(t):
+        return {"a": t, "r": []}
+
+    def need(q, sem, val):
+        if known[q].get(sem, 0) < val:
+            eng[q].wait_ge(T.sem[sem], val)
+            known[q][sem] = val
+
+    def access(q, outs, ins, tok, dma):
+        todo = {}
+        acc = [(r, True) for o in outs for r in o["r"]] + [(r, False) for o in ins for r in o["r"]]
+        for (n, a0, a1, b0, b1, bs), wr in acc:
+            ps = n.startswith("ps")
+            for (m0, m1, n0, n1, ns, pw, pq, pd, (sem, val)) in log.get(n, []):
+                if known[q].get(sem, 0) >= val: continue
+                if not ps and (m0 >= a1 or m1 <= a0 or n0 >= b1 or n1 <= b0 or (bs == ns and (b0 - n0) % bs)): continue
+                if pd or dma or pq != q: hit = pw or wr or (ps and pq != q)
+                else: hit = (pw or wr) and q != "T"
+                if hit: todo[sem] = max(todo.get(sem, 0), cnt[sem] if pd else val)
+        for s, val in todo.items(): need(q, s, val)
+        for (n, a0, a1, b0, b1, bs), wr in acc:
+            keep = [o for o in log.get(n, []) if not (
+                a0 <= o[0] and o[1] <= a1 and b0 <= o[2] and o[3] <= b1 and (bs == 1 or (bs == o[4] and (b0 - o[2]) % bs == 0))
+                and (wr or (not o[5] and o[6] == q and not o[7] and not dma)))]
+            log[n] = keep + [(a0, a1, b0, b1, bs, wr, q, dma, tok)]
+
+    def call(q, outs, ins, fn):
+        s = csem[q]
+        access(q, outs, ins, (s, cnt.get(s, 0) + 1), False)
+        fn().then_inc(T.sem[s], 1)
+        cnt[s] = cnt.get(s, 0) + 1
+
+    def dma(q, sem, out, in_):
+        access(q, [out], [in_], (sem, cnt.get(sem, 0) + 16), True)
+        eng[q].dma_start(out["a"], in_["a"]).then_inc(T.sem[sem], 16)
+        cnt[sem] = cnt.get(sem, 0) + 16
+
+    def arg(s):
+        return s["a"] if isinstance(s, dict) else s
+
+    def ins(*xs):
+        return [x for x in xs if isinstance(x, dict)]
+
+    def tc(out, in_):
+        call("V", [{"r": out["r"][:1]}], [{"r": out["r"][1:]}, in_], lambda: g.vector.tensor_copy(out["a"], in_["a"]))
+
+    def tt(out, a, b, op):
+        call("V", [out], [a, b], lambda: g.vector.tensor_tensor(out["a"], a["a"], b["a"], op))
+
+    def ts(out, a, s1, s2, op0, op1=None):
+        if op1 is None: call("V", [out], ins(a, s1), lambda: g.vector.tensor_scalar(out["a"], a["a"], arg(s1), None, op0))
+        else: call("V", [out], ins(a, s1, s2), lambda: g.vector.tensor_scalar(out["a"], a["a"], arg(s1), arg(s2), op0, op1))
+
+    def fill(out, x):
+        call("V", [out], [], lambda: g.vector.memset(out["a"], x))
+
+    def act(out, in_, func=F.Identity, bias=0.0, scale=1.0):
+        call("S", [out], ins(in_, bias, scale), lambda: g.scalar.activation(out["a"], in_["a"], func, bias=arg(bias), scale=arg(scale)))
+
+    def acopy(out, in_):
+        call("S", [out], [in_], lambda: g.scalar.activation(out["a"], in_["a"], F.Copy))
+
+    def quant(q, z, in_):
+        call("V", [q, z], [in_], lambda: g.vector.quantize_mx(q["a"], z["a"], in_["a"]))
+
+    def mm(out, w, wz, x, xz):
+        call("T", [out], [w, wz, x, xz], lambda: g.tensor.matmul_mx(out["a"], w["a"], wz["a"], x["a"], xz["a"], True, True))
+
+    def iota(out, pattern, base=0, cm=0, exact=False):
+        if exact: call("G", [out], [], lambda: g.iota(out["a"], pattern, base, cm))
+        else: call("G", [out], [], lambda: g.iota(out["a"], pattern, base, cm, allow_small_or_imprecise_dtypes=True))
+
+    def diag(in_, n):
+        tt(v("dg", 0, n), in_, v("mask", 0, n), A.mult)
+        call("V", [v("ds", 0, n)], [v("res", 0, n), v("dg", 0, n)],
+             lambda: g.vector.tensor_tensor_scan(T.ds[:, 0:n], T.res[:, 0:n], T.dg[:, 0:n], 0.0, A.mult, A.add))
+        return v("ds", 15, n, 16)
+
+    for k in range(8): dma("Y", "dl", v("lw", p0=16 * k, p1=16 * k + 16), ext(T.ln[:, :]))
+    dma("Y", "dp", v("pw"), ext(T.p[:, :]))
+    dma("S", "dxn", v("xn"), ext(T.x[:, :]))
+    dma("Y", "du", v("ut", 96, 512), ext(T.u[:, 96:512]))
+    for r in range(3):
+        for i in range(3): dma("Y", "du", v("ut", 32 * r + 8 * i, 32 * r + 8 * i + 8), ext(T.u[:, 64 * i:64 * i + 8]))
+        dma("Y", "du", v("ut", 32 * r + 24, 32 * r + 32), ext(T.u[:, 0:8]))
+    for i in range(16): dma("Y", "dxt", v("xt", p0=8 * i, p1=8 * i + 8), ext(T.x[i:128:16, :]))
+    dma("Y", "dw", cb(v("wq")), ext(T.wc[:, :]))
+    dma("Y", "dw", v("wz"), ext(T.ws[:, :]))
+    dma("Y", "dv", v("vt"), ext(T.v[:, :]))
+
+    col = [0]
+
+    def newcol():
+        col[0] += 1
+        return v("cols", col[0] - 1, col[0])
+
+    iota(v("pci", 0, 1), [[1, 1]], 0, 1, True)
+    iota(v("k16"), [[64, 4]])
+    iota(v("m16"), [[0, 20], [1, 16]])
+    iota(v("iot"), [[1, 320]])
+    iota(v("lbr"), [[1, 64], [640, 4]], 256)
+    iota(v("wli"), [[128, 4], [2, 8]])
+    gcol, icol, pcol, i8, lk, half = [newcol() for _ in range(6)]
+    pc = lambda k: v("pci", k, k + 1)
+    ts(pc(1), pc(0), 4, None, A.arith_shift_right)
+    ts(pc(2), pc(0), 15, None, A.bitwise_and)
+    ts(pc(3), pc(0), 7, None, A.bitwise_and)
+    ts(pc(4), pc(0), 5, None, A.arith_shift_right)
+    tc(pcol, pc(0)); ts(half, pc(0), 16.0, None, A.is_ge)
+    fill(v("tlF", p1=32), 0.0)
+    tc(gcol, pc(1)); tc(icol, pc(2)); tc(i8, pc(3)); ts(lk, pc(4), 256.0, None, A.add)
+    ts(v("hb"), v("k16"), 0.0, half, A.mult, A.add)
+    fill(v("tlI", p1=32), 0.0)
+
+    W = {"F": _weights(False), "I": _weights(True)}
+    for d in "FI":
+        for (p, slot, link), ws in W[d][0].items():
+            todo = {}
+            for a in range(4): todo.setdefault((ws[2 * a], ws[2 * a + 1]), []).append(a)
+            for (w0, w1), as_ in todo.items():
+                if w0 == w1 == 0: continue
+                c, n = (link * 4 + slot) * 128 + p, "tl" + d
+                if len(as_) == 4: act(v(n, c, c + 97, 32, p1=32), v("hb", p1=32), bias=float(w0), scale=float(w1 - w0))
+                else:
+                    for a in as_: act(v(n, c + 32 * a, c + 32 * a + 1, p1=32), v("hb", 0, 1, p1=32), bias=float(w0), scale=float(w1 - w0))
+
+    def weigh(d):
+        call("V", [v("tr", p1=32)], [v("tl" + d, p1=32)], lambda: g.vector.transpose(T.tr[0:32, :], T["tl" + d][0:32, :]))
+        for k in range(8):
+            o, i = v("ab" + d, 512 * (k // 4) + k % 4, 512 * (k // 4) + 512, 4, p1=32), v("tr", 128 * k, 128 * k + 128, p1=32)
+            if k % 2: acopy(o, i)
+            else: tc(o, i)
+        quant(v("aq" + d), v("az" + d), v("ab" + d))
+
+    ts(v("mask"), v("m16"), icol, None, A.is_equal)
+    ts(v("res"), v("m16"), 0.0, None, A.not_equal)
+    fill(v("abF"), 0.0)
+    fill(v("eb"), 0.0)
+
+    tc(v("l16"), v("lw"))
+    L = [v("l16", 16 * i, 16 * i + 16) for i in range(3)]
+    AF = [v("af", 256 * i, 256 * i + 256) for i in range(5)]
+    AL = [v("al16", 16 * i, 16 * i + 16) for i in range(5)]
+    row = v("iot", 0, 256)
+    for i in range(3): tc(ind(AF[i], L[i]), row)
+    tc(v("cc", 0, 256), ind(AF[0], L[1]))
+    tc(ind(AF[3], L[2]), v("cc", 0, 256))
+    for i in (2, 3, 1, 0): tc(AL[i], diag(AF[i], 256))
+
+    thr, t3 = newcol(), newcol()
+    ts(thr, i8, 6.0, 1e29, A.is_ge, A.mult)
+    ts(t3, pcol, 24.0, 1e29, A.is_ge, A.mult)
+    quant(v("uq"), v("uz"), v("ut"))
+    quant(v("xq", 0, 256), v("xz", 0, 256), v("xn", 0, 1024))
+    tt(thr, thr, t3, A.max)
+    ST = [AL[2], AL[3], AL[1], AL[0]]
+
+    def signs():
+        mm(v("ps0", 0, 256), v("uq"), v("uz"), v("xq", 0, 256), v("xz", 0, 256))
+        ts(v("sg"), v("ps0", 0, 256), thr, None, A.is_gt)
+        for t in range(4):
+            o, w = v("nt", t, 1024, 4), ind(v("sg"), ST[t])
+            if t < 2: tc(o, w)
+            else: acopy(o, w)
+        quant(v("nq"), v("nz"), v("nt"))
+
+    signs()
+    weigh("F")
+
+    t0, t1, t2 = newcol(), newcol(), newcol()
+    ts(t0, gcol, 512.0, 6144.0, A.mult, A.add)
+    ts(t1, gcol, 768.0, -512.0, A.mult, A.add)
+    ts(t2, gcol, 320.0, None, A.mult)
+    tc(v("p16"), v("pw"))
+    tc(ind(v("pv"), v("p16")), v("iot"))
+    ts(v("atr", 0, 128), v("iot", 0, 128), 4.0, t0, A.mult, A.add)
+    ts(v("atr", 128, 320), v("iot", 128, 320), 4.0, t1, A.mult, A.add)
+    tc(v("pi16"), diag(v("pv"), 320))
+    tc(ind(v("atf"), v("pi16")), v("atr"))
+
+    def spread(sem, dram, src, dst):
+        for h in range(8): dma("Y", sem, v(dram, 320 * h, 320 * h + 320, p0=0, p1=16), v(src, p0=16 * h, p1=16 * h + 16))
+        for k in range(8): dma("Y", sem, v(dst, p0=16 * k, p1=16 * k + 16), v(dram, p0=0, p1=16))
+
+    def window(qs, sem, src, off, base, w):
+        for k in range(8):
+            dma(qs[k % len(qs)], sem, v("win", base, base + 8 * w, p0=16 * k, p1=16 * k + 16), v(src, off, off + w))
+
+    window(["Y"], "dbB", "xt", 0, 6144, 512)
+    window(["Y"], "dbA", "xt", 512, 0, 768)
+    spread("dt1", "tabd", "atf", "tab1")
+
+    tc(ind(v("v2", 0, 256), AL[2]), row)
+    ts(v("v2", 256, 320), v("iot", 0, 64), 4.0, lk, A.mult, A.add)
+    LB = [v("lbf", 256 * i, 256 * i + 256) for i in range(3)]
+    LG = [v("lg", 256 * i, 256 * i + 256) for i in range(3)]
+    LGI = [v("lgi", 256 * i, 256 * i + 256) for i in range(3)]
+    for i in range(2): tc(ind(LB[i], AL[i]), v("lbr"))
+
+    def base(d, orig, near, mid, last, one, zero, midl, share):
+        lb = v("lbr")
+        s = [(lb, 0), (lb, 0), (last, 0), (last, 7), (lb, 1), (lb, 1), (lb, 1), (lb, 1),
+             (mid, 1), (mid, 1), (midl, 0), (midl, 1), (mid, 6), (mid, 6), (mid, 6), (mid, 6)] + [(orig, h) for h in range(8)]
+        s += [(one, 0), (one, 0), (near, 0), (near, 7), (one, 1), (one, 1), (zero, 0), (zero, 1)]
+        late = (10, 11, 24, 25, 28, 29, 30, 31)
+        for n, k in enumerate([k for k in range(32) if k not in late] + list(late)):
+            out, o, b = v("base" + d, k, 8192, 32), s[k][0], float(320 * s[k][1])
+            if n % share: act(out, o, bias=b)
+            else: ts(out, o, b, None, A.add)
+
+    acopy(LG[0], ind(LB[1], AL[2]))
+    acopy(LG[1], ind(LB[0], AL[2]))
+    acopy(LG[2], ind(LB[0], AL[1]))
+    base("F", AF[2], AF[3], AF[1], AF[0], LG[0], LG[1], LG[2], 3)
+
+    tc(v("w2"), diag(ind(v("v2"), v("pi16")), 320))
+    tc(v("n16F"), v("w2"))
+    ts(v("ty"), v("w2"), 256.0, None, A.is_ge)
+    ts(v("q32F"), v("ty"), -256.0, None, A.mult)
+    tt(v("q32F"), v("q32F"), v("w2"), A.add)
+    ts(v("q32F"), v("q32F"), 32.0, None, A.mult)
+
+    def consts(b):
+        for k in range(8):
+            ts(v("steps", k, k + 1), gcol, float(k), float(b[k] - (b[k - 1] if k else 0)), A.is_ge, A.mult)
+        c = newcol()
+        call("V", [c], [v("steps", 0, 8)], lambda: g.vector.tensor_reduce(c["a"], T.steps[:, 0:8], AxisListType.X, A.add))
+        return c
+
+    bs, bl, dif = consts(W["F"][1][0]), consts(W["F"][1][1]), newcol()
+    tt(dif, bl, bs, A.subtract)
+    ts(v("biF"), v("ty"), dif, bs, A.mult, A.add)
+
+    def layer_constants():
+        t4, t5, tg = newcol(), newcol(), newcol()
+        ts(t5, icol, 8.0, None, A.is_ge)
+        ts(t4, i8, 16.0, t5, A.mult, A.add)
+        ts(tg, icol, 8.0, gcol, A.mult, A.add)
+        ts(v("wl16"), v("wli"), t4, None, A.add)
+        for b in range(4): ts(v("eb", 513 * b, 512 * b + 512, 4), v("iot", 0, 128), tg, None, A.is_equal)
+        acopy(v("wpz"), ind(v("wz"), v("wl16")))
+        tc(cw(v("wp")), ind(cw(v("wq")), v("wl16")))
+        quant(v("eq"), v("ez"), v("eb"))
+
+    def places(d):
+        mm(v("ps1", 0, 256), v("aq" + d, 0, 128), v("az" + d, 0, 128), v("nq"), v("nz"))
+        mm(v("ps2", 0, 256), v("aq" + d, 128, 256), v("az" + d, 128, 256), v("nq"), v("nz"))
+        tc(v("ntb", 0, 256), v("ps1", 0, 256))
+        acopy(v("ntb", 256, 512), v("ps2", 0, 256))
+        N, n = v("ni"), diag(ind(v("ntb"), v("n16" + d)), 320)
+        tt(N, n, v("bi" + d), A.add)
+        fb = lambda k, e=None: v("fb", 20 * k, 20 * (e or k + 1))
+        ts(fb(0), N, 7, None, A.bitwise_and)
+        ts(fb(1), N, 19, None, A.arith_shift_right)
+        for k, sh, m in ((2, 3, 15), (3, 14, 31), (4, 7, 1), (5, 11, 1), (6, 13, 1)):
+            ts(fb(k), N, sh, m, A.arith_shift_right, A.bitwise_and)
+        G, E = v("gb", 0, 40), v("gb", 40, 60)
+        tt(G, fb(2, 4), fb(0, 2), A.subtract)
+        tt(G, G, fb(4, 6), A.mult)
+        tt(G, G, fb(0, 2), A.add)
+        tt(E, v("gb", 0, 20), v("gb", 20, 40), A.subtract)
+        tt(E, E, fb(6), A.mult)
+        tt(E, E, v("gb", 20, 40), A.add)
+        tt(E, E, v("q32" + d), A.add)
+        tc(v("ix"), E)
+        tc(v("pl"), diag(ind(v("base" + d), v("ix")), 320))
+
+    def offsets(dst, lst):
+        for t in range(4): ts(v(dst, 20 * t, 20 * t + 20), lst, float(t), None, A.add)
+
+    def gather(tile, ofs, a, b):
+        for t in range(4):
+            o, w = v(tile, 4 * a + t, 4 * b, 4), ind(v("win"), v(ofs, 20 * t + a // 16, 20 * t + b // 16))
+            if t < 2: tc(o, w)
+            else: acopy(o, w)
+
+    def inverse_places():
+        tc(v("nt", 1, 1024, 4), ind(v("sg"), AL[4]))
+        quant(v("nq"), v("nz"), v("nt"))
+        places("I")
+        tc(v("tf"), ind(v("tab1"), v("pl")))
+
+    def layer(q, z, qc, n, off, dst):
+        for b in range(4):
+            mm(v("ps%d" % b, 0, n), v("wp", 128 * b, 128 * b + 128), v("wpz", 128 * b, 128 * b + 128), v(q, qc, qc + n), v(z, qc, qc + n))
+            mm(v("ps%d" % (4 + b), 0, n), v("eq", 128 * b, 128 * b + 128), v("ez", 128 * b, 128 * b + 128), v(q, qc, qc + n), v(z, qc, qc + n))
+            o = v("rl", 320 * b + off, 320 * b + off + n)
+            act(o, v("ps%d" % b, 0, n), F.Relu, scale=0.015625)
+            tt(v(dst, b, 4 * n, 4), o, v("ps%d" % (4 + b), 0, n), A.add)
+
+    for r in range(3):
+        if r: signs()
+        places("F")
+        offsets("ofz", diag(ind(v("tab2" if r else "tab1"), v("pl")), 320))
+        gather("zg", "ofz", 0, 128)
+        quant(v("zq", 0, 128), v("zz", 0, 128), v("zg", 0, 512))
+        dst = T.cores[rank ^ (1 << r)]
+        rid, pid, _ = topo.addr(dst)
+        engines = topo.engines(core, dst)[:8]
+        m, n, arr = sum(1 << e for e in engines), len(engines), "ar%d" % r
+        for to, fr in (("lc%d" % r, "zq"), ("lz%d" % r, "zz")):
+            o, i = v(to), v(fr, 0, 128)
+            if fr == "zq": o, i = cb(o), cb(i)
+            access("G", [], [i], ("snt", cnt.get("snt", 0) + n), True)
+            g.remote_dma(o["a"], i["a"], T.sem[arr], T.sem.snt, pid, rid, m)
+            cnt["snt"] = cnt.get("snt", 0) + n
+            cnt[arr] = cnt.get(arr, 0) + n
+            log[to] = [(0, 128, 0, 128, 1, True, "R", True, (arr, cnt[arr]))]
+        gather("zg", "ofz", 128, 320)
+        quant(v("zq", 128, 320), v("zz", 128, 320), v("zg", 512, 1280))
+        if r == 0: layer_constants()
+        layer("zq", "zz", 128, 192, 0, "ya")
+        window(["Y"], "dbA", "ya", 0, 0, 768)
+        if r == 2:
+            tc(v("opb"), ind(v("tabp"), v("pl")))
+            dma("Y", "do", ext(T.op[:, :]), v("opb", ps=16))
+        if r > 0: inverse_places()
+        if r == 0:
+            fill(v("abI"), 0.0)
+            tc(v("cc", 256, 512), ind(AF[2], L[1]))
+            tc(ind(AF[4], L[0]), v("cc", 256, 512))
+            tc(ind(LB[2], AL[2]), v("lbr"))
+            tc(AL[4], diag(AF[4], 256))
+        if r == 1: spread("dt1", "tabd", "tf", "tab2")
+        layer("lc%d" % r, "lz%d" % r, 0, 128, 192, "yb")
+        window(["Y", "S"], "dbB", "yb", 0, 6144, 512)
+        if r == 0:
+            for k, (i, j) in enumerate(((1, 0), (2, 0), (2, 1))): acopy(LGI[k], ind(LB[i], AL[j]))
+            base("I", AF[0], AF[4], AF[1], AF[2], LGI[0], LGI[1], LGI[2], 2)
+            weigh("I")
+            bs, bl = consts(W["I"][1][0]), consts(W["I"][1][1])
+            i4c, q4 = newcol(), newcol()
+            ts(i4c, icol, 4.0, lk, A.mult, A.add)
+            ts(v("biI", 0, 16), v("iot", 0, 16), 0.0, bs, A.mult, A.add)
+            ts(v("biI", 16, 20), v("iot", 0, 4), 0.0, bl, A.mult, A.add)
+            ts(q4, i4c, -256.0, None, A.add)
+            tc(v("n16I", 0, 16), v("lw", 0, 16))
+            ts(v("n16I", 16, 20), v("k16"), i4c, None, A.add)
+            ts(v("q32I", 0, 16), v("lw", 0, 16), 32.0, None, A.mult)
+            ts(v("q32I", 16, 20), v("k16"), q4, 32.0, A.add, A.mult)
+            inverse_places()
+            spread("dt1", "tabd", "tf", "tab2")
+        offsets("ofx", diag(ind(v("tf"), v("pi16")), 320))
+        if r == 2: quant(v("vq"), v("vz"), v("vt"))
+        n = 320 if r == 2 else 256
+        gather("xg", "ofx", 0, n)
+        quant(v("xq", 0, n), v("xz", 0, n), v("xg", 0, 4 * n))
+        if r == 1:
+            ts(v("apr"), v("iot"), t2, None, A.add)
+            tc(ind(v("apf"), v("pi16")), v("apr"))
+            spread("dt2", "tabpd", "apf", "tabp")
+    mm(v("ps0", 0, 320), v("vq"), v("vz"), v("xq"), v("xz"))
+    dma("Y", "do", ext(T.oc[:, :]), cb(v("xq")))
+    for k in range(4): dma("S", "do", ext(T.osc[4 * k:4 * k + 4, :]), v("xz", p0=32 * k, p1=32 * k + 4))
+    tc(v("yo"), v("ps0", 0, 320))
+    dma("Y", "do", ext(T.y[:, :]), v("yo"))
+    for s, n in cnt.items(): need("G", s, n)

@@ -1,4 +1,4 @@
-from concourse.mybir import dt, AluOpType as A, AxisListType, ActivationFunctionType as F
+from concourse.mybir import dt, AluOpType as A, ActivationFunctionType as F
 
 f4, bf, u2, i4, X4, u1 = "float32", "bfloat16", "uint16", "int32", "float8_e4m3fn_x4", "uint8"
 SCRATCH = {}
@@ -13,7 +13,7 @@ _add("sbuf", bf, ut=512, vt=512, xn=1280, xt=1280, eb=2048, abF=1024, abI=1024, 
      win=10240, sg=256, tlF=1024, tlI=1024, tr=1024)
 _add("sbuf", X4, wq=512, wp=512, uq=128, vq=128, eq=512, aqF=256, aqI=256, xq=320, zq=320, nq=256, lc0=128, lc1=128, lc2=128)
 _add("sbuf", u1, wz=512, wpz=512, uz=128, vz=128, ez=512, azF=256, azI=256, xz=320, zz=320, nz=256, lz0=128, lz1=128, lz2=128)
-_add("sbuf", f4, iot=320, lbr=256, m16=320, mask=320, res=320, dg=320, ds=320, cols=64, steps=32, wli=32, k16=4, pv=320, atr=320,
+_add("sbuf", f4, iot=320, lbr=256, m16=320, mask=320, res=320, dg=320, ds=320, cols=64, wli=32, k16=4, pv=320, atr=320,
      apr=320, atf=320, apf=320, tab1=2560, tab2=2560, tabp=2560, af=1280, cc=512, v2=320, lbf=768, lg=768, lgi=768, baseF=8192,
      baseI=8192, ntb=512, tf=320, rl=1280, yo=320, opb=320, hb=4, w2=20, ty=20, q32F=20, q32I=20, biF=20, biI=20)
 _add("sbuf", i4, lw=48, pw=20, pci=8, ni=20, fb=140, gb=60)
@@ -179,9 +179,6 @@ def rank_program(g, core, T, topo):
         for i in range(3): dma("Y", "du", v("ut", 32 * r + 8 * i, 32 * r + 8 * i + 8), ext(T.u[:, 64 * i:64 * i + 8]))
         dma("Y", "du", v("ut", 32 * r + 24, 32 * r + 32), ext(T.u[:, 0:8]))
     for i in range(16): dma("Y", "dxt", v("xt", p0=8 * i, p1=8 * i + 8), ext(T.x[i:128:16, :]))
-    dma("Y", "dw", cb(v("wq")), ext(T.wc[:, :]))
-    dma("Y", "dw", v("wz"), ext(T.ws[:, :]))
-    dma("Y", "dv", v("vt"), ext(T.v[:, :]))
 
     col = [0]
 
@@ -189,13 +186,27 @@ def rank_program(g, core, T, topo):
         col[0] += 1
         return v("cols", col[0] - 1, col[0])
 
+    W = {"F": _weights(False), "I": _weights(True)}
+
+    def consts(b):
+        c = newcol()
+        iota(c, [[0, 1]], int(b[7]))
+        for k in range(6, -1, -1):
+            if b[k] != b[k + 1]: call("G", [c], [c], lambda: g.affine_select(c["a"], c["a"], [[0, 1]], A.is_ge, float(b[k]), -16 * (k + 1), 1))
+        return c
+
     iota(v("pci", 0, 1), [[1, 1]], 0, 1, True)
     iota(v("k16"), [[64, 4]])
     iota(v("m16"), [[0, 20], [1, 16]])
     iota(v("iot"), [[1, 320]])
     iota(v("lbr"), [[1, 64], [640, 4]], 256)
     iota(v("wli"), [[128, 4], [2, 8]])
-    gcol, icol, pcol, i8, lk, half = [newcol() for _ in range(6)]
+    iota(v("abF"), [[0, 1024]])
+    iota(v("eb"), [[0, 2048]])
+    CB = {"F": [consts(W["F"][1][t]) for t in (0, 1)]}
+    iota(v("abI"), [[0, 1024]])
+    CB["I"] = [consts(W["I"][1][t]) for t in (0, 1)]
+    gcol, icol, pcol, i8, lk, half, t0, t1, t2 = [newcol() for _ in range(9)]
     pc = lambda k: v("pci", k, k + 1)
     ts(pc(1), pc(0), 4, None, A.arith_shift_right)
     ts(pc(2), pc(0), 15, None, A.bitwise_and)
@@ -206,9 +217,13 @@ def rank_program(g, core, T, topo):
     tc(gcol, pc(1)); tc(icol, pc(2)); tc(i8, pc(3)); ts(lk, pc(4), 256.0, None, A.add)
     ts(v("hb"), v("k16"), 0.0, half, A.mult, A.add)
     fill(v("tlI", p1=32), 0.0)
+    ts(t0, gcol, 512.0, 6144.0, A.mult, A.add)
+    ts(t1, gcol, 768.0, -512.0, A.mult, A.add)
+    ts(t2, gcol, 320.0, None, A.mult)
+    ts(v("mask"), v("m16"), icol, None, A.is_equal)
+    ts(v("res"), v("m16"), 0.0, None, A.not_equal)
 
-    W = {"F": _weights(False), "I": _weights(True)}
-    for d in "FI":
+    def weights(d):
         for (p, slot, link), ws in W[d][0].items():
             todo = {}
             for a in range(4): todo.setdefault((ws[2 * a], ws[2 * a + 1]), []).append(a)
@@ -227,20 +242,60 @@ def rank_program(g, core, T, topo):
             else: tc(o, i)
         quant(v("aq" + d), v("az" + d), v("ab" + d))
 
-    ts(v("mask"), v("m16"), icol, None, A.is_equal)
-    ts(v("res"), v("m16"), 0.0, None, A.not_equal)
-    fill(v("abF"), 0.0)
-    fill(v("eb"), 0.0)
+    weights("F")
 
-    tc(v("l16"), v("lw"))
     L = [v("l16", 16 * i, 16 * i + 16) for i in range(3)]
     AF = [v("af", 256 * i, 256 * i + 256) for i in range(5)]
     AL = [v("al16", 16 * i, 16 * i + 16) for i in range(5)]
+    LB = [v("lbf", 256 * i, 256 * i + 256) for i in range(3)]
+    LG = [v("lg", 256 * i, 256 * i + 256) for i in range(3)]
+    LGI = [v("lgi", 256 * i, 256 * i + 256) for i in range(3)]
     row = v("iot", 0, 256)
-    for i in range(3): tc(ind(AF[i], L[i]), row)
-    tc(v("cc", 0, 256), ind(AF[0], L[1]))
-    tc(ind(AF[3], L[2]), v("cc", 0, 256))
-    for i in (2, 3, 1, 0): tc(AL[i], diag(AF[i], 256))
+    tc(v("l16"), v("lw"))
+    tc(v("p16"), v("pw"))
+    for i in (0, 1, 2): tc(ind(AF[i], L[i]), row)
+    act(v("atr", 0, 128), v("iot", 0, 128), bias=t0, scale=4.0)
+    act(v("atr", 128, 320), v("iot", 128, 320), bias=t1, scale=4.0)
+    acopy(v("atf"), ind(v("atr"), v("p16")))
+
+    def spread(sem, dram, src, dst, hops=3):
+        for h in range(8 if hops & 1 else 0): dma("Y", sem, v(dram, 320 * h, 320 * h + 320, p0=0, p1=16), v(src, p0=16 * h, p1=16 * h + 16))
+        for k in range(8 if hops & 2 else 0): dma("Y", sem, v(dst, p0=16 * k, p1=16 * k + 16), v(dram, p0=0, p1=16))
+
+    def window(qs, sem, src, off, base, w):
+        for k in range(8):
+            dma(qs[k % len(qs)], sem, v("win", base, base + 8 * w, p0=16 * k, p1=16 * k + 16), v(src, off, off + w))
+
+    spread("dt1", "tabd", "atf", "tab1", 1)
+    window(["Y"], "dbB", "xt", 0, 6144, 512)
+    spread("dt1", "tabd", "atf", "tab1", 2)
+    window(["Y"], "dbA", "xt", 512, 0, 768)
+    dma("Y", "dw", cb(v("wq")), ext(T.wc[:, :]))
+    dma("Y", "dw", v("wz"), ext(T.ws[:, :]))
+    dma("Y", "dv", v("vt"), ext(T.v[:, :]))
+
+    def base(d, orig, near, mid, last, one, zero, midl, part):
+        lb = v("lbr")
+        s = [(lb, 0), (lb, 0), (last, 0), (last, 7), (lb, 1), (lb, 1), (lb, 1), (lb, 1),
+             (mid, 1), (mid, 1), (midl, 0), (midl, 1), (mid, 6), (mid, 6), (mid, 6), (mid, 6)] + [(orig, h) for h in range(8)]
+        s += [(one, 0), (one, 0), (near, 0), (near, 7), (one, 1), (one, 1), (zero, 0), (zero, 1)]
+        late = [26, 27, 24, 25, 28, 29, 30, 31, 10, 11]
+        for n, k in enumerate(([k for k in range(32) if k not in late] + late)[part]):
+            out, o, b = v("base" + d, k, 8192, 32), s[k][0], float(320 * s[k][1])
+            if (n % 2 and d == "I") or (n % 3 == 2 and part.start > 16): ts(out, o, b, None, A.add)
+            else: act(out, o, bias=b)
+
+    def baseF(a, b):
+        base("F", AF[2], AF[3], AF[1], AF[0], LG[0], LG[1], LG[2], slice(a, b))
+
+    baseF(0, 8)
+    acopy(v("cc", 0, 256), ind(AF[0], L[1]))
+    for i in range(3): acopy(LB[i], ind(v("lbr"), L[i]))
+    tc(AL[2], diag(AF[2], 256))
+    acopy(AF[3], ind(v("cc", 0, 256), AL[2]))
+    acopy(v("v2", 0, 256), ind(row, L[2]))
+    for i in (1, 0, 3): tc(AL[i], diag(AF[i], 256))
+    baseF(8, 14)
 
     thr, t3 = newcol(), newcol()
     ts(thr, i8, 6.0, 1e29, A.is_ge, A.mult)
@@ -250,92 +305,45 @@ def rank_program(g, core, T, topo):
     tt(thr, thr, t3, A.max)
     ST = [AL[2], AL[3], AL[1], AL[0]]
 
-    def signs():
+    def signs(between=None):
         mm(v("ps0", 0, 256), v("uq"), v("uz"), v("xq", 0, 256), v("xz", 0, 256))
         ts(v("sg"), v("ps0", 0, 256), thr, None, A.is_gt)
         for t in range(4):
             o, w = v("nt", t, 1024, 4), ind(v("sg"), ST[t])
             if t < 2: tc(o, w)
             else: acopy(o, w)
+        if between: between()
         quant(v("nq"), v("nz"), v("nt"))
 
-    signs()
-    weigh("F")
+    def layer_constants():
+        t4, t5, tg = newcol(), newcol(), newcol()
+        ts(t5, icol, 8.0, None, A.is_ge)
+        ts(tg, icol, 8.0, gcol, A.mult, A.add)
+        ts(t4, i8, 16.0, t5, A.mult, A.add)
+        for b in range(4): ts(v("eb", 513 * b, 512 * b + 512, 4), v("iot", 0, 128), tg, None, A.is_equal)
+        ts(v("wl16"), v("wli"), t4, None, A.add)
+        tc(cw(v("wp")), ind(cw(v("wq")), v("wl16")))
+        acopy(v("wpz"), ind(v("wz"), v("wl16")))
+        quant(v("eq"), v("ez"), v("eb"))
 
-    t0, t1, t2 = newcol(), newcol(), newcol()
-    ts(t0, gcol, 512.0, 6144.0, A.mult, A.add)
-    ts(t1, gcol, 768.0, -512.0, A.mult, A.add)
-    ts(t2, gcol, 320.0, None, A.mult)
-    tc(v("p16"), v("pw"))
+    signs(lambda: weigh("F"))
     tc(ind(v("pv"), v("p16")), v("iot"))
-    ts(v("atr", 0, 128), v("iot", 0, 128), 4.0, t0, A.mult, A.add)
-    ts(v("atr", 128, 320), v("iot", 128, 320), 4.0, t1, A.mult, A.add)
     tc(v("pi16"), diag(v("pv"), 320))
-    tc(ind(v("atf"), v("pi16")), v("atr"))
-
-    def spread(sem, dram, src, dst):
-        for h in range(8): dma("Y", sem, v(dram, 320 * h, 320 * h + 320, p0=0, p1=16), v(src, p0=16 * h, p1=16 * h + 16))
-        for k in range(8): dma("Y", sem, v(dst, p0=16 * k, p1=16 * k + 16), v(dram, p0=0, p1=16))
-
-    def window(qs, sem, src, off, base, w):
-        for k in range(8):
-            dma(qs[k % len(qs)], sem, v("win", base, base + 8 * w, p0=16 * k, p1=16 * k + 16), v(src, off, off + w))
-
-    window(["Y"], "dbB", "xt", 0, 6144, 512)
-    window(["Y"], "dbA", "xt", 512, 0, 768)
-    spread("dt1", "tabd", "atf", "tab1")
-
-    tc(ind(v("v2", 0, 256), AL[2]), row)
-    ts(v("v2", 256, 320), v("iot", 0, 64), 4.0, lk, A.mult, A.add)
-    LB = [v("lbf", 256 * i, 256 * i + 256) for i in range(3)]
-    LG = [v("lg", 256 * i, 256 * i + 256) for i in range(3)]
-    LGI = [v("lgi", 256 * i, 256 * i + 256) for i in range(3)]
-    for i in range(2): tc(ind(LB[i], AL[i]), v("lbr"))
-
-    def base(d, orig, near, mid, last, one, zero, midl, share):
-        lb = v("lbr")
-        s = [(lb, 0), (lb, 0), (last, 0), (last, 7), (lb, 1), (lb, 1), (lb, 1), (lb, 1),
-             (mid, 1), (mid, 1), (midl, 0), (midl, 1), (mid, 6), (mid, 6), (mid, 6), (mid, 6)] + [(orig, h) for h in range(8)]
-        s += [(one, 0), (one, 0), (near, 0), (near, 7), (one, 1), (one, 1), (zero, 0), (zero, 1)]
-        late = (10, 11, 24, 25, 28, 29, 30, 31)
-        for n, k in enumerate([k for k in range(32) if k not in late] + list(late)):
-            out, o, b = v("base" + d, k, 8192, 32), s[k][0], float(320 * s[k][1])
-            if n % share: act(out, o, bias=b)
-            else: ts(out, o, b, None, A.add)
-
     acopy(LG[0], ind(LB[1], AL[2]))
     acopy(LG[1], ind(LB[0], AL[2]))
     acopy(LG[2], ind(LB[0], AL[1]))
-    base("F", AF[2], AF[3], AF[1], AF[0], LG[0], LG[1], LG[2], 3)
-
+    baseF(14, 17)
+    baseF(17, 32)
+    ts(v("v2", 256, 320), v("iot", 0, 64), 4.0, lk, A.mult, A.add)
     tc(v("w2"), diag(ind(v("v2"), v("pi16")), 320))
     tc(v("n16F"), v("w2"))
     ts(v("ty"), v("w2"), 256.0, None, A.is_ge)
     ts(v("q32F"), v("ty"), -256.0, None, A.mult)
     tt(v("q32F"), v("q32F"), v("w2"), A.add)
-    ts(v("q32F"), v("q32F"), 32.0, None, A.mult)
-
-    def consts(b):
-        for k in range(8):
-            ts(v("steps", k, k + 1), gcol, float(k), float(b[k] - (b[k - 1] if k else 0)), A.is_ge, A.mult)
-        c = newcol()
-        call("V", [c], [v("steps", 0, 8)], lambda: g.vector.tensor_reduce(c["a"], T.steps[:, 0:8], AxisListType.X, A.add))
-        return c
-
-    bs, bl, dif = consts(W["F"][1][0]), consts(W["F"][1][1]), newcol()
+    bs, bl, dif = CB["F"][0], CB["F"][1], newcol()
     tt(dif, bl, bs, A.subtract)
+    ts(v("q32F"), v("q32F"), 32.0, None, A.mult)
     ts(v("biF"), v("ty"), dif, bs, A.mult, A.add)
-
-    def layer_constants():
-        t4, t5, tg = newcol(), newcol(), newcol()
-        ts(t5, icol, 8.0, None, A.is_ge)
-        ts(t4, i8, 16.0, t5, A.mult, A.add)
-        ts(tg, icol, 8.0, gcol, A.mult, A.add)
-        ts(v("wl16"), v("wli"), t4, None, A.add)
-        for b in range(4): ts(v("eb", 513 * b, 512 * b + 512, 4), v("iot", 0, 128), tg, None, A.is_equal)
-        acopy(v("wpz"), ind(v("wz"), v("wl16")))
-        tc(cw(v("wp")), ind(cw(v("wq")), v("wl16")))
-        quant(v("eq"), v("ez"), v("eb"))
 
     def places(d):
         mm(v("ps1", 0, 256), v("aq" + d, 0, 128), v("az" + d, 0, 128), v("nq"), v("nz"))
@@ -386,6 +394,7 @@ def rank_program(g, core, T, topo):
     for r in range(3):
         if r: signs()
         places("F")
+        if r == 0: weights("I")
         offsets("ofz", diag(ind(v("tab2" if r else "tab1"), v("pl")), 320))
         gather("zg", "ofz", 0, 128)
         quant(v("zq", 0, 128), v("zz", 0, 128), v("zg", 0, 512))
@@ -409,21 +418,17 @@ def rank_program(g, core, T, topo):
         if r == 2:
             tc(v("opb"), ind(v("tabp"), v("pl")))
             dma("Y", "do", ext(T.op[:, :]), v("opb", ps=16))
-        if r > 0: inverse_places()
         if r == 0:
-            fill(v("abI"), 0.0)
-            tc(v("cc", 256, 512), ind(AF[2], L[1]))
-            tc(ind(AF[4], L[0]), v("cc", 256, 512))
-            tc(ind(LB[2], AL[2]), v("lbr"))
+            acopy(v("cc", 256, 512), ind(AF[2], L[1]))
+            acopy(AF[4], ind(v("cc", 256, 512), AL[0]))
+            for k, (i, j) in enumerate(((1, 0), (2, 0), (2, 1))): acopy(LGI[k], ind(LB[i], AL[j]))
             tc(AL[4], diag(AF[4], 256))
-        if r == 1: spread("dt1", "tabd", "tf", "tab2")
+            weigh("I")
         layer("lc%d" % r, "lz%d" % r, 0, 128, 192, "yb")
         window(["Y", "S"], "dbB", "yb", 0, 6144, 512)
         if r == 0:
-            for k, (i, j) in enumerate(((1, 0), (2, 0), (2, 1))): acopy(LGI[k], ind(LB[i], AL[j]))
-            base("I", AF[0], AF[4], AF[1], AF[2], LGI[0], LGI[1], LGI[2], 2)
-            weigh("I")
-            bs, bl = consts(W["I"][1][0]), consts(W["I"][1][1])
+            base("I", AF[0], AF[4], AF[1], AF[2], LGI[0], LGI[1], LGI[2], slice(0, 32))
+            bs, bl = CB["I"]
             i4c, q4 = newcol(), newcol()
             ts(i4c, icol, 4.0, lk, A.mult, A.add)
             ts(v("biI", 0, 16), v("iot", 0, 16), 0.0, bs, A.mult, A.add)
@@ -433,16 +438,16 @@ def rank_program(g, core, T, topo):
             ts(v("n16I", 16, 20), v("k16"), i4c, None, A.add)
             ts(v("q32I", 0, 16), v("lw", 0, 16), 32.0, None, A.mult)
             ts(v("q32I", 16, 20), v("k16"), q4, 32.0, A.add, A.mult)
-            inverse_places()
-            spread("dt1", "tabd", "tf", "tab2")
+        inverse_places()
+        if r < 2: spread("dt1", "tabd", "tf", "tab2")
         offsets("ofx", diag(ind(v("tf"), v("pi16")), 320))
         if r == 2: quant(v("vq"), v("vz"), v("vt"))
         n = 320 if r == 2 else 256
         gather("xg", "ofx", 0, n)
         quant(v("xq", 0, n), v("xz", 0, n), v("xg", 0, 4 * n))
         if r == 1:
-            ts(v("apr"), v("iot"), t2, None, A.add)
-            tc(ind(v("apf"), v("pi16")), v("apr"))
+            act(v("apr"), v("iot"), bias=t2)
+            acopy(v("apf"), ind(v("apr"), v("p16")))
             spread("dt2", "tabpd", "apf", "tabp")
     mm(v("ps0", 0, 320), v("vq"), v("vz"), v("xq"), v("xz"))
     dma("Y", "do", ext(T.oc[:, :]), cb(v("xq")))

from concourse.mybir import dt, AluOpType as A, ActivationFunctionType as F

f4, bf, u2, i4, X4, u1 = "float32", "bfloat16", "uint16", "int32", "float8_e4m3fn_x4", "uint8"
SCRATCH = {}


def _add(where, dtype, **kw):
    for k, n in kw.items():
        SCRATCH[k] = (where, n if isinstance(n, list) else [128, n], dtype)


_add("sbuf", bf, ut=512, vt=512, xn=1280, xt=1280, eb=2048, abF=1024, abI=1024, xg=1280, zg=1280, nt=1024, ya=768, yb=512,
     win=10240, sg=256, tlF=1024, tlI=1024, tr=1024)
_add("sbuf", X4, wq=512, wp=512, uq=128, vq=128, eq=512, aqF=256, aqI=256, xq=320, zq=320, nq=256, lc0=128, lc1=128, lc2=128)
_add("sbuf", u1, wz=512, wpz=512, uz=128, vz=128, ez=512, azF=256, azI=256, xz=320, zz=320, nz=256, lz0=128, lz1=128, lz2=128)
_add("sbuf", f4, iot=320, lbr=256, m16=320, mask=320, res=320, dg=320, ds=320, cols=64, wli=32, k16=4, pv=320, atr=320,
     apr=320, atf=320, apf=320, tab1=2560, tab2=2560, tabp=2560, af=1280, cc=512, v2=320, lbf=768, lg=768, lgi=768, baseF=8192,
     baseI=8192, ntb=512, tf=320, rl=1280, yo=320, opb=320, hb=4, w2=20, ty=20, q32F=20, q32I=20, biF=20, biI=20)
_add("sbuf", i4, lw=48, pw=20, pci=8, ni=20, fb=140, gb=60)
_add("sbuf", u2, l16=48, p16=20, pi16=20, al16=80, n16F=20, n16I=20, wl16=32, ix=20, pl=20, ofz=80, ofx=80)
_add("dram", f4, tabd=[16, 2560], tabpd=[16, 2560])
_add("psum", f4, **{"ps%d" % b: 512 for b in range(8)})
DSEM = ["dp", "dl", "du", "dv", "dxn", "dxt", "dw", "dbA", "dbB", "dt1", "dt2", "do"]
SEMAPHORES = ["sv", "ss", "st", "sg", "snt", "ar0", "ar1", "ar2"] + DSEM


def _fields(g, link):
    e, b = {}, [0]

    def add(c, k, i, K, w):
        e[c, k, i, K] = e.get((c, k, i, K), 0) + w

    add(0, "s", 0, 3, 1); add(0, "b", 0, 3, -2); b[0] += 2
    add(0, "b", 0, 2, 8); add(0, "s", 0, 2, 16); add(0, "s", 1, 2, 16); b[0] += 64
    add(1, "b", 1, 2, -128); b[0] += 128
    beta = g % 2
    if link: b[0] += 130 * beta
    else: add(0, "b", 2, 0, 2); add(1, "b", 2, 0, 128)
    if link or g in (1, 6):
        add(2, "s", 0, 1, 1 << 14); add(2, "b", 1, 0, 1 << 15); add(2, "b", 0, 1, -(1 << 15)); b[0] += 26 << 14
    elif g in (0, 2, 5, 7):
        add(2, "b", 0, 0, 1 << 14); b[0] += 30 << 14
    else: b[0] += 24 << 14
    if link:
        add(1, "s", 1, 0, 2048); add(1, "s", 2, 0, 2048)
        add(1, "b", 2, 0, -8192 if beta else 8192); b[0] += 8192 * beta
        add(2, "s", 0, 0, -(1 << 20)); add(2, "s", 2, 0, 5 << 19); b[0] += 18 << 19
    else:
        w, c = {0: ((1, 1, -1), 2), 7: ((-1, -1, 1), 3), 1: ((0, 1, 1), 2), 6: ((0, -1, -1), 4),
                2: ((1, 1, 1), 1), 5: ((-1, -1, -1), 4)}.get(g, ((0, 0, 0), 0))
        for i in range(3):
            if w[i]: add(1, "s", i, 0, 512 * w[i])
            add(2, "s", i, 0, -(1 << 20))
        b[0] += 512 * c + ((g + 19) << 19)
        if g == 0: add(1, "s", 2, 0, 8192)
        if g == 7: add(1, "s", 2, 0, -8192); b[0] += 8192
    return e, b[0]


def _weights(inverse):
    w, bias = {}, [[0] * 8, [0] * 8]
    for link in (0, 1):
        for g in range(8):
            e, b = _fields(g, link)
            for (c, k, i, K), x in e.items():
                slot, j = K, i
                if inverse:
                    slot, j = (3, 1, 2, 0)[K], 2 - i
                    if k == "s": b += x; x = -x
                w.setdefault((8 * c + 2 * j + (k == "b"), slot, link), [0] * 8)[g] += x
            bias[link][g] = b
    return w, bias


def rank_program(g, core, T, topo):
    rank = T.rank_of(core)
    if rank is None:
        return
    eng = {"V": g.vector, "S": g.scalar, "T": g.tensor, "G": g, "Y": g.sync}
    csem = {"V": "sv", "S": "ss", "T": "st", "G": "sg"}
    cnt, known, log = {}, {q: {} for q in eng}, {}

    def v(name, c0=0, c1=None, cs=1, p0=0, p1=128, ps=1):
        if c1 is None: c1 = SCRATCH[name][1][1]
        return {"a": T[name][p0:p1:ps, c0:c1:cs], "r": [(name, p0, p1, c0, c1, cs)]}

    def ind(w, o):
        return {"a": w["a"].indirect(o["a"]), "r": w["r"] + o["r"]}

    def cb(w):
        return {"a": w["a"].bitcast(dt.uint8), "r": w["r"]}

    def cw(w):
        return {"a": w["a"].bitcast(dt.uint32), "r": w["r"]}

    def ext(t):
        return {"a": t, "r": []}

    def need(q, sem, val):
        if known[q].get(sem, 0) < val:
            eng[q].wait_ge(T.sem[sem], val)
            known[q][sem] = val

    def access(q, outs, ins, tok, dma):
        todo = {}
        acc = [(r, True) for o in outs for r in o["r"]] + [(r, False) for o in ins for r in o["r"]]
        for (n, a0, a1, b0, b1, bs), wr in acc:
            ps = n.startswith("ps")
            for (m0, m1, n0, n1, ns, pw, pq, pd, (sem, val)) in log.get(n, []):
                if known[q].get(sem, 0) >= val: continue
                if not ps and (m0 >= a1 or m1 <= a0 or n0 >= b1 or n1 <= b0 or (bs == ns and (b0 - n0) % bs)): continue
                if pd or dma or pq != q: hit = pw or wr or (ps and pq != q)
                else: hit = (pw or wr) and q != "T"
                if hit: todo[sem] = max(todo.get(sem, 0), cnt[sem] if pd else val)
        for s, val in todo.items(): need(q, s, val)
        for (n, a0, a1, b0, b1, bs), wr in acc:
            keep = [o for o in log.get(n, []) if not (
                a0 <= o[0] and o[1] <= a1 and b0 <= o[2] and o[3] <= b1 and (bs == 1 or (bs == o[4] and (b0 - o[2]) % bs == 0))
                and (wr or (not o[5] and o[6] == q and not o[7] and not dma)))]
            log[n] = keep + [(a0, a1, b0, b1, bs, wr, q, dma, tok)]

    def call(q, outs, ins, fn):
        s = csem[q]
        access(q, outs, ins, (s, cnt.get(s, 0) + 1), False)
        fn().then_inc(T.sem[s], 1)
        cnt[s] = cnt.get(s, 0) + 1

    def dma(q, sem, out, in_):
        access(q, [out], [in_], (sem, cnt.get(sem, 0) + 16), True)
        eng[q].dma_start(out["a"], in_["a"]).then_inc(T.sem[sem], 16)
        cnt[sem] = cnt.get(sem, 0) + 16

    def arg(s):
        return s["a"] if isinstance(s, dict) else s

    def ins(*xs):
        return [x for x in xs if isinstance(x, dict)]

    def tc(out, in_):
        call("V", [{"r": out["r"][:1]}], [{"r": out["r"][1:]}, in_], lambda: g.vector.tensor_copy(out["a"], in_["a"]))

    def tt(out, a, b, op):
        call("V", [out], [a, b], lambda: g.vector.tensor_tensor(out["a"], a["a"], b["a"], op))

    def ts(out, a, s1, s2, op0, op1=None):
        if op1 is None: call("V", [out], ins(a, s1), lambda: g.vector.tensor_scalar(out["a"], a["a"], arg(s1), None, op0))
        else: call("V", [out], ins(a, s1, s2), lambda: g.vector.tensor_scalar(out["a"], a["a"], arg(s1), arg(s2), op0, op1))

    def fill(out, x):
        call("V", [out], [], lambda: g.vector.memset(out["a"], x))

    def act(out, in_, func=F.Identity, bias=0.0, scale=1.0):
        call("S", [out], ins(in_, bias, scale), lambda: g.scalar.activation(out["a"], in_["a"], func, bias=arg(bias), scale=arg(scale)))

    def acopy(out, in_):
        call("S", [out], [in_], lambda: g.scalar.activation(out["a"], in_["a"], F.Copy))

    def quant(q, z, in_):
        call("V", [q, z], [in_], lambda: g.vector.quantize_mx(q["a"], z["a"], in_["a"]))

    def mm(out, w, wz, x, xz):
        call("T", [out], [w, wz, x, xz], lambda: g.tensor.matmul_mx(out["a"], w["a"], wz["a"], x["a"], xz["a"], True, True))

    def iota(out, pattern, base=0, cm=0, exact=False):
        if exact: call("G", [out], [], lambda: g.iota(out["a"], pattern, base, cm))
        else: call("G", [out], [], lambda: g.iota(out["a"], pattern, base, cm, allow_small_or_imprecise_dtypes=True))

    def diag(in_, n):
        tt(v("dg", 0, n), in_, v("mask", 0, n), A.mult)
        call("V", [v("ds", 0, n)], [v("res", 0, n), v("dg", 0, n)],
             lambda: g.vector.tensor_tensor_scan(T.ds[:, 0:n], T.res[:, 0:n], T.dg[:, 0:n], 0.0, A.mult, A.add))
        return v("ds", 15, n, 16)

    for k in range(8): dma("Y", "dl", v("lw", p0=16 * k, p1=16 * k + 16), ext(T.ln[:, :]))
    dma("Y", "dp", v("pw"), ext(T.p[:, :]))
    dma("S", "dxn", v("xn"), ext(T.x[:, :]))
    dma("Y", "du", v("ut", 96, 512), ext(T.u[:, 96:512]))
    for r in range(3):
        for i in range(3): dma("Y", "du", v("ut", 32 * r + 8 * i, 32 * r + 8 * i + 8), ext(T.u[:, 64 * i:64 * i + 8]))
        dma("Y", "du", v("ut", 32 * r + 24, 32 * r + 32), ext(T.u[:, 0:8]))
    for i in range(16): dma("Y", "dxt", v("xt", p0=8 * i, p1=8 * i + 8), ext(T.x[i:128:16, :]))

    col = [0]

    def newcol():
        col[0] += 1
        return v("cols", col[0] - 1, col[0])

    W = {"F": _weights(False), "I": _weights(True)}

    def consts(b):
        c = newcol()
        iota(c, [[0, 1]], int(b[7]))
        for k in range(6, -1, -1):
            if b[k] != b[k + 1]: call("G", [c], [c], lambda: g.affine_select(c["a"], c["a"], [[0, 1]], A.is_ge, float(b[k]), -16 * (k + 1), 1))
        return c

    iota(v("pci", 0, 1), [[1, 1]], 0, 1, True)
    iota(v("k16"), [[64, 4]])
    iota(v("m16"), [[0, 20], [1, 16]])
    iota(v("iot"), [[1, 320]])
    iota(v("lbr"), [[1, 64], [640, 4]], 256)
    iota(v("wli"), [[128, 4], [2, 8]])
    iota(v("abF"), [[0, 1024]])
    iota(v("eb"), [[0, 2048]])
    CB = {"F": [consts(W["F"][1][t]) for t in (0, 1)]}
    iota(v("abI"), [[0, 1024]])
    CB["I"] = [consts(W["I"][1][t]) for t in (0, 1)]
    gcol, icol, pcol, i8, lk, half, t0, t1, t2 = [newcol() for _ in range(9)]
    pc = lambda k: v("pci", k, k + 1)
    ts(pc(1), pc(0), 4, None, A.arith_shift_right)
    ts(pc(2), pc(0), 15, None, A.bitwise_and)
    ts(pc(3), pc(0), 7, None, A.bitwise_and)
    ts(pc(4), pc(0), 5, None, A.arith_shift_right)
    tc(pcol, pc(0)); ts(half, pc(0), 16.0, None, A.is_ge)
    fill(v("tlF", p1=32), 0.0)
    tc(gcol, pc(1)); tc(icol, pc(2)); tc(i8, pc(3)); ts(lk, pc(4), 256.0, None, A.add)
    ts(v("hb"), v("k16"), 0.0, half, A.mult, A.add)
    fill(v("tlI", p1=32), 0.0)
    ts(t0, gcol, 512.0, 6144.0, A.mult, A.add)
    ts(t1, gcol, 768.0, -512.0, A.mult, A.add)
    ts(t2, gcol, 320.0, None, A.mult)
    ts(v("mask"), v("m16"), icol, None, A.is_equal)
    ts(v("res"), v("m16"), 0.0, None, A.not_equal)

    def weights(d):
        for (p, slot, link), ws in W[d][0].items():
            todo = {}
            for a in range(4): todo.setdefault((ws[2 * a], ws[2 * a + 1]), []).append(a)
            for (w0, w1), as_ in todo.items():
                if w0 == w1 == 0: continue
                c, n = (link * 4 + slot) * 128 + p, "tl" + d
                if len(as_) == 4: act(v(n, c, c + 97, 32, p1=32), v("hb", p1=32), bias=float(w0), scale=float(w1 - w0))
                else:
                    for a in as_: act(v(n, c + 32 * a, c + 32 * a + 1, p1=32), v("hb", 0, 1, p1=32), bias=float(w0), scale=float(w1 - w0))

    def weigh(d):
        call("V", [v("tr", p1=32)], [v("tl" + d, p1=32)], lambda: g.vector.transpose(T.tr[0:32, :], T["tl" + d][0:32, :]))
        for k in range(8):
            o, i = v("ab" + d, 512 * (k // 4) + k % 4, 512 * (k // 4) + 512, 4, p1=32), v("tr", 128 * k, 128 * k + 128, p1=32)
            if k % 2: acopy(o, i)
            else: tc(o, i)
        quant(v("aq" + d), v("az" + d), v("ab" + d))

    weights("F")

    L = [v("l16", 16 * i, 16 * i + 16) for i in range(3)]
    AF = [v("af", 256 * i, 256 * i + 256) for i in range(5)]
    AL = [v("al16", 16 * i, 16 * i + 16) for i in range(5)]
    LB = [v("lbf", 256 * i, 256 * i + 256) for i in range(3)]
    LG = [v("lg", 256 * i, 256 * i + 256) for i in range(3)]
    LGI = [v("lgi", 256 * i, 256 * i + 256) for i in range(3)]
    row = v("iot", 0, 256)
    tc(v("l16"), v("lw"))
    tc(v("p16"), v("pw"))
    for i in (0, 1, 2): tc(ind(AF[i], L[i]), row)
    act(v("atr", 0, 128), v("iot", 0, 128), bias=t0, scale=4.0)
    act(v("atr", 128, 320), v("iot", 128, 320), bias=t1, scale=4.0)
    acopy(v("atf"), ind(v("atr"), v("p16")))

    def spread(sem, dram, src, dst, hops=3):
        for h in range(8 if hops & 1 else 0): dma("Y", sem, v(dram, 320 * h, 320 * h + 320, p0=0, p1=16), v(src, p0=16 * h, p1=16 * h + 16))
        for k in range(8 if hops & 2 else 0): dma("Y", sem, v(dst, p0=16 * k, p1=16 * k + 16), v(dram, p0=0, p1=16))

    def window(qs, sem, src, off, base, w):
        for k in range(8):
            dma(qs[k % len(qs)], sem, v("win", base, base + 8 * w, p0=16 * k, p1=16 * k + 16), v(src, off, off + w))

    spread("dt1", "tabd", "atf", "tab1", 1)
    window(["Y"], "dbB", "xt", 0, 6144, 512)
    spread("dt1", "tabd", "atf", "tab1", 2)
    window(["Y"], "dbA", "xt", 512, 0, 768)
    dma("Y", "dw", cb(v("wq")), ext(T.wc[:, :]))
    dma("Y", "dw", v("wz"), ext(T.ws[:, :]))
    dma("Y", "dv", v("vt"), ext(T.v[:, :]))

    def base(d, orig, near, mid, last, one, zero, midl, part):
        lb = v("lbr")
        s = [(lb, 0), (lb, 0), (last, 0), (last, 7), (lb, 1), (lb, 1), (lb, 1), (lb, 1),
             (mid, 1), (mid, 1), (midl, 0), (midl, 1), (mid, 6), (mid, 6), (mid, 6), (mid, 6)] + [(orig, h) for h in range(8)]
        s += [(one, 0), (one, 0), (near, 0), (near, 7), (one, 1), (one, 1), (zero, 0), (zero, 1)]
        late = [26, 27, 24, 25, 28, 29, 30, 31, 10, 11]
        for n, k in enumerate(([k for k in range(32) if k not in late] + late)[part]):
            out, o, b = v("base" + d, k, 8192, 32), s[k][0], float(320 * s[k][1])
            if (n % 2 and d == "I") or (n % 3 == 2 and part.start > 16): ts(out, o, b, None, A.add)
            else: act(out, o, bias=b)

    def baseF(a, b):
        base("F", AF[2], AF[3], AF[1], AF[0], LG[0], LG[1], LG[2], slice(a, b))

    baseF(0, 8)
    acopy(v("cc", 0, 256), ind(AF[0], L[1]))
    for i in range(3): acopy(LB[i], ind(v("lbr"), L[i]))
    tc(AL[2], diag(AF[2], 256))
    acopy(AF[3], ind(v("cc", 0, 256), AL[2]))
    acopy(v("v2", 0, 256), ind(row, L[2]))
    for i in (1, 0, 3): tc(AL[i], diag(AF[i], 256))
    baseF(8, 14)

    thr, t3 = newcol(), newcol()
    ts(thr, i8, 6.0, 1e29, A.is_ge, A.mult)
    ts(t3, pcol, 24.0, 1e29, A.is_ge, A.mult)
    quant(v("uq"), v("uz"), v("ut"))
    quant(v("xq", 0, 256), v("xz", 0, 256), v("xn", 0, 1024))
    tt(thr, thr, t3, A.max)
    ST = [AL[2], AL[3], AL[1], AL[0]]

    def signs(between=None):
        mm(v("ps0", 0, 256), v("uq"), v("uz"), v("xq", 0, 256), v("xz", 0, 256))
        ts(v("sg"), v("ps0", 0, 256), thr, None, A.is_gt)
        for t in range(4):
            o, w = v("nt", t, 1024, 4), ind(v("sg"), ST[t])
            if t < 2: tc(o, w)
            else: acopy(o, w)
        if between: between()
        quant(v("nq"), v("nz"), v("nt"))

    def layer_constants():
        t4, t5, tg = newcol(), newcol(), newcol()
        ts(t5, icol, 8.0, None, A.is_ge)
        ts(tg, icol, 8.0, gcol, A.mult, A.add)
        ts(t4, i8, 16.0, t5, A.mult, A.add)
        for b in range(4): ts(v("eb", 513 * b, 512 * b + 512, 4), v("iot", 0, 128), tg, None, A.is_equal)
        ts(v("wl16"), v("wli"), t4, None, A.add)
        tc(cw(v("wp")), ind(cw(v("wq")), v("wl16")))
        acopy(v("wpz"), ind(v("wz"), v("wl16")))
        quant(v("eq"), v("ez"), v("eb"))

    signs(lambda: weigh("F"))
    tc(ind(v("pv"), v("p16")), v("iot"))
    tc(v("pi16"), diag(v("pv"), 320))
    acopy(LG[0], ind(LB[1], AL[2]))
    acopy(LG[1], ind(LB[0], AL[2]))
    acopy(LG[2], ind(LB[0], AL[1]))
    baseF(14, 17)
    baseF(17, 32)
    ts(v("v2", 256, 320), v("iot", 0, 64), 4.0, lk, A.mult, A.add)
    tc(v("w2"), diag(ind(v("v2"), v("pi16")), 320))
    tc(v("n16F"), v("w2"))
    ts(v("ty"), v("w2"), 256.0, None, A.is_ge)
    ts(v("q32F"), v("ty"), -256.0, None, A.mult)
    tt(v("q32F"), v("q32F"), v("w2"), A.add)
    bs, bl, dif = CB["F"][0], CB["F"][1], newcol()
    tt(dif, bl, bs, A.subtract)
    ts(v("q32F"), v("q32F"), 32.0, None, A.mult)
    ts(v("biF"), v("ty"), dif, bs, A.mult, A.add)

    def places(d):
        mm(v("ps1", 0, 256), v("aq" + d, 0, 128), v("az" + d, 0, 128), v("nq"), v("nz"))
        mm(v("ps2", 0, 256), v("aq" + d, 128, 256), v("az" + d, 128, 256), v("nq"), v("nz"))
        tc(v("ntb", 0, 256), v("ps1", 0, 256))
        acopy(v("ntb", 256, 512), v("ps2", 0, 256))
        N, n = v("ni"), diag(ind(v("ntb"), v("n16" + d)), 320)
        tt(N, n, v("bi" + d), A.add)
        fb = lambda k, e=None: v("fb", 20 * k, 20 * (e or k + 1))
        ts(fb(0), N, 7, None, A.bitwise_and)
        ts(fb(1), N, 19, None, A.arith_shift_right)
        for k, sh, m in ((2, 3, 15), (3, 14, 31), (4, 7, 1), (5, 11, 1), (6, 13, 1)):
            ts(fb(k), N, sh, m, A.arith_shift_right, A.bitwise_and)
        G, E = v("gb", 0, 40), v("gb", 40, 60)
        tt(G, fb(2, 4), fb(0, 2), A.subtract)
        tt(G, G, fb(4, 6), A.mult)
        tt(G, G, fb(0, 2), A.add)
        tt(E, v("gb", 0, 20), v("gb", 20, 40), A.subtract)
        tt(E, E, fb(6), A.mult)
        tt(E, E, v("gb", 20, 40), A.add)
        tt(E, E, v("q32" + d), A.add)
        tc(v("ix"), E)
        tc(v("pl"), diag(ind(v("base" + d), v("ix")), 320))

    def offsets(dst, lst):
        for t in range(4): ts(v(dst, 20 * t, 20 * t + 20), lst, float(t), None, A.add)

    def gather(tile, ofs, a, b):
        for t in range(4):
            o, w = v(tile, 4 * a + t, 4 * b, 4), ind(v("win"), v(ofs, 20 * t + a // 16, 20 * t + b // 16))
            if t < 2: tc(o, w)
            else: acopy(o, w)

    def inverse_places():
        tc(v("nt", 1, 1024, 4), ind(v("sg"), AL[4]))
        quant(v("nq"), v("nz"), v("nt"))
        places("I")
        tc(v("tf"), ind(v("tab1"), v("pl")))

    def layer(q, z, qc, n, off, dst):
        for b in range(4):
            mm(v("ps%d" % b, 0, n), v("wp", 128 * b, 128 * b + 128), v("wpz", 128 * b, 128 * b + 128), v(q, qc, qc + n), v(z, qc, qc + n))
            mm(v("ps%d" % (4 + b), 0, n), v("eq", 128 * b, 128 * b + 128), v("ez", 128 * b, 128 * b + 128), v(q, qc, qc + n), v(z, qc, qc + n))
            o = v("rl", 320 * b + off, 320 * b + off + n)
            act(o, v("ps%d" % b, 0, n), F.Relu, scale=0.015625)
            tt(v(dst, b, 4 * n, 4), o, v("ps%d" % (4 + b), 0, n), A.add)

    for r in range(3):
        if r: signs()
        places("F")
        if r == 0: weights("I")
        offsets("ofz", diag(ind(v("tab2" if r else "tab1"), v("pl")), 320))
        gather("zg", "ofz", 0, 128)
        quant(v("zq", 0, 128), v("zz", 0, 128), v("zg", 0, 512))
        dst = T.cores[rank ^ (1 << r)]
        rid, pid, _ = topo.addr(dst)
        engines = topo.engines(core, dst)[:8]
        m, n, arr = sum(1 << e for e in engines), len(engines), "ar%d" % r
        for to, fr in (("lc%d" % r, "zq"), ("lz%d" % r, "zz")):
            o, i = v(to), v(fr, 0, 128)
            if fr == "zq": o, i = cb(o), cb(i)
            access("G", [], [i], ("snt", cnt.get("snt", 0) + n), True)
            g.remote_dma(o["a"], i["a"], T.sem[arr], T.sem.snt, pid, rid, m)
            cnt["snt"] = cnt.get("snt", 0) + n
            cnt[arr] = cnt.get(arr, 0) + n
            log[to] = [(0, 128, 0, 128, 1, True, "R", True, (arr, cnt[arr]))]
        gather("zg", "ofz", 128, 320)
        quant(v("zq", 128, 320), v("zz", 128, 320), v("zg", 512, 1280))
        if r == 0: layer_constants()
        layer("zq", "zz", 128, 192, 0, "ya")
        window(["Y"], "dbA", "ya", 0, 0, 768)
        if r == 2:
            tc(v("opb"), ind(v("tabp"), v("pl")))
            dma("Y", "do", ext(T.op[:, :]), v("opb", ps=16))
        if r == 0:
            acopy(v("cc", 256, 512), ind(AF[2], L[1]))
            acopy(AF[4], ind(v("cc", 256, 512), AL[0]))
            for k, (i, j) in enumerate(((1, 0), (2, 0), (2, 1))): acopy(LGI[k], ind(LB[i], AL[j]))
            tc(AL[4], diag(AF[4], 256))
            weigh("I")
        layer("lc%d" % r, "lz%d" % r, 0, 128, 192, "yb")
        window(["Y", "S"], "dbB", "yb", 0, 6144, 512)
        if r == 0:
            base("I", AF[0], AF[4], AF[1], AF[2], LGI[0], LGI[1], LGI[2], slice(0, 32))
            bs, bl = CB["I"]
            i4c, q4 = newcol(), newcol()
            ts(i4c, icol, 4.0, lk, A.mult, A.add)
            ts(v("biI", 0, 16), v("iot", 0, 16), 0.0, bs, A.mult, A.add)
            ts(v("biI", 16, 20), v("iot", 0, 4), 0.0, bl, A.mult, A.add)
            ts(q4, i4c, -256.0, None, A.add)
            tc(v("n16I", 0, 16), v("lw", 0, 16))
            ts(v("n16I", 16, 20), v("k16"), i4c, None, A.add)
            ts(v("q32I", 0, 16), v("lw", 0, 16), 32.0, None, A.mult)
            ts(v("q32I", 16, 20), v("k16"), q4, 32.0, A.add, A.mult)
        inverse_places()
        if r < 2: spread("dt1", "tabd", "tf", "tab2")
        offsets("ofx", diag(ind(v("tf"), v("pi16")), 320))
        if r == 2: quant(v("vq"), v("vz"), v("vt"))
        n = 320 if r == 2 else 256
        gather("xg", "ofx", 0, n)
        quant(v("xq", 0, n), v("xz", 0, n), v("xg", 0, 4 * n))
        if r == 1:
            act(v("apr"), v("iot"), bias=t2)
            acopy(v("apf"), ind(v("apr"), v("p16")))
            spread("dt2", "tabpd", "apf", "tabp")
    mm(v("ps0", 0, 320), v("vq"), v("vz"), v("xq"), v("xz"))
    dma("Y", "do", ext(T.oc[:, :]), cb(v("xq")))
    for k in range(4): dma("S", "do", ext(T.osc[4 * k:4 * k + 4, :]), v("xz", p0=32 * k, p1=32 * k + 4))
    tc(v("yo"), v("ps0", 0, 320))
    dma("Y", "do", ext(T.y[:, :]), v("yo"))
    for s, n in cnt.items(): need("G", s, n)
